import numpy as np
import ml_dtypes


def mxq(x, axis, fmt="e4m3"):
    dtype, down = {"e4m3": (ml_dtypes.float8_e4m3fn, 7), "e5m2": (ml_dtypes.float8_e5m2, 14)}[fmt]
    v = np.moveaxis(np.asarray(x, np.float32).astype(ml_dtypes.bfloat16).astype(np.float64), axis, -1)
    blocks = v.reshape(v.shape[:-1] + (-1, 32))
    amax = np.abs(blocks).max(-1, keepdims=True)
    byte = np.maximum(np.where(amax > 0, np.frexp(amax)[1] - 1 + 127, 0) - down, 1)
    scale = np.exp2(byte - 127.0)
    codes = (blocks / scale).astype(np.float32).astype(dtype).astype(np.float64)
    return np.moveaxis((codes * scale).reshape(v.shape), -1, axis)


WIDE = False


def mx_kscale(k):
    if not WIDE:
        return np.ones(k)
    levels = np.array([10, -10, 5, -5, 0])
    if k % 512:
        return np.exp2(np.random.permutation(np.resize(levels, k // 32))).repeat(32)
    a = np.empty((k // 512, 16))
    for p in range(k // 512):
        a[p, :8] = np.random.permutation(np.resize(levels, 8))
        for g in range(8):
            far = levels[np.abs(levels - a[p, g]) >= 10]
            a[p, g + 8] = far[np.random.randint(len(far))]
    return np.exp2(a.ravel()).repeat(32)


def f64(x):
    return np.asarray(x).astype(np.float64)


def striped(idx):
    return np.tile(idx.reshape(-1, 16).T, (8, 1)).astype(np.uint16)


def unstriped(offs):
    return offs[:16].T.reshape(-1).astype(np.int64)


K, T, E, C, N = 512, 512, 8, 128, 128


def by_expert(wq, xq):
    return np.concatenate([wq[e].T @ xq[:, e * C:(e + 1) * C] for e in range(E)], axis=1)


def setup_inputs():
    n = np.random.standard_normal
    s = mx_kscale(K)[:, None]
    first = np.random.permutation(np.repeat(np.arange(E), T // E))
    second = (first + 1 + np.random.permutation(np.repeat(np.arange(E - 1), -(-T // (E - 1)))[:T])) % E
    while np.bincount(second, minlength=E).max() != T // E:
        load = np.bincount(second, minlength=E); hi, lo = int(load.argmax()), int(load.argmin())
        t = np.flatnonzero((second == hi) & (first != lo))[0]; second[t] = lo
    slot_token = np.empty(E * C, np.int64); pos = np.empty((2, T), np.int64); fill = np.zeros(E, np.int64)
    place = np.stack([np.random.permutation(C) for _ in range(E)])
    for r, deal in enumerate((first, second)):
        for t in np.random.permutation(T):
            e = deal[t]; j = e * C + place[e, fill[e]]; fill[e] += 1; slot_token[j] = t; pos[r, t] = j
    g = np.random.uniform(0.2, 0.8, T)
    return {
        "xT": (n((K, T)) * s).astype(np.float32),
        "w": (n((E, K, N)) / np.sqrt(K) / s[None]).astype(np.float32),
        "gate": np.stack([np.tile(g, (N, 1)), np.tile(1.0 - g, (N, 1))]).astype(np.float32),
        "offs": striped(slot_token),
        "pos1": striped(pos[0]),
        "pos2": striped(pos[1]),
    }


def reference(xT, w, gate, offs, pos1, pos2):
    idx = unstriped(offs)
    xq = mxq(f64(xT)[:, idx], 0, "e4m3")
    y = by_expert(mxq(f64(w), 1, "e4m3"), xq)
    return f64(gate[0]) * y[:, unstriped(pos1)] + f64(gate[1]) * y[:, unstriped(pos2)]

@@ -1,0 +1,140 @@
+from contextlib import ExitStack
+
+import concourse.mybir as mybir
+
+K, T, E, C, N = 512, 512, 8, 128, 128
+FLOPS = 2 * K * N * E * C
+
+F32 = mybir.dt.float32
+BF16 = mybir.dt.bfloat16
+U32 = mybir.dt.uint32
+U16 = mybir.dt.uint16
+U8 = mybir.dt.uint8
+FP8X4 = mybir.dt.float8_e4m3fn_x4
+MULT = mybir.AluOpType.mult
+ADD = mybir.AluOpType.add
+
+P = 128
+PACK = 4
+SLOTS = E * C
+CUT = 256
+N_CUTS = SLOTS // CUT
+HALF = T // 2
+
+
+def tile_routed_moe_kernel(tc, xT, w, gate, offs, pos1, pos2, out):
+    nc = tc.nc
+    with ExitStack() as ctx:
+        lists = ctx.enter_context(tc.tile_pool(name="lists", bufs=1))
+        keep = ctx.enter_context(tc.tile_pool(name="keep", bufs=1))
+        psum = ctx.enter_context(tc.psum_pool(name="psum", bufs=1))
+
+        offs_t = lists.tile([P, SLOTS // 16], U16, name="offs_t")
+        pos1_t = lists.tile([P, T // 16], U16, name="pos1_t")
+        pos2_t = lists.tile([P, T // 16], U16, name="pos2_t")
+
+        warm_in = keep.tile([P, 1], F32, name="warm_in")
+        warm_out = keep.tile([P, 1], F32, name="warm_out")
+        nc.vector.memset(warm_in[:], 0.0)
+        nc.scalar.copy(warm_out[:], warm_in[:])
+
+        nc.sync.dma_start(offs_t[:], offs)
+        planes = xT.rearrange("(p t) n -> p t n", t=PACK)
+        xp = []
+        for t in range(PACK):
+            plane = keep.tile([P, T], F32, name="xp%d" % t)
+            nc.sync.dma_start(plane[:], planes[:, t, :])
+            xp.append(plane)
+        w_raw = []
+        for c in range(N_CUTS):
+            raw = keep.tile([P, 2, PACK, N], F32, name="w_raw%d" % c)
+            nc.sync.dma_start(
+                raw[:].rearrange("p e j n -> p e (j n)"),
+                w[2 * c : 2 * c + 2].rearrange("e (p j) n -> p e (j n)", j=PACK),
+            )
+            w_raw.append(raw)
+        nc.sync.dma_start(pos1_t[:], pos1)
+        nc.sync.dma_start(pos2_t[:], pos2)
+        gates = []
+        for r in range(2):
+            g = keep.tile([P, T], F32, name="gate%d" % r)
+            nc.sync.dma_start(g[:], gate[r])
+            gates.append(g)
+
+        w_codes = keep.tile([P, SLOTS], U32, name="w_codes", align_bytes=64)
+        w_scales = keep.tile([P, SLOTS], U8, name="w_scales", align_bytes=64)
+        x_codes = keep.tile([P, SLOTS], U32, name="x_codes", align_bytes=64)
+        x_scales = keep.tile([P, SLOTS], U8, name="x_scales", align_bytes=64)
+        y = keep.tile([P, SLOTS], F32, name="y")
+
+        g4s, xgs, wgs = {}, {}, {}
+
+        def gather(s):
+            g4 = keep.tile([P, PACK, CUT], F32, name="g4_%d" % s)
+            for t in range(PACK):
+                nc.vector.tensor_copy(
+                    g4[:, t, :], xp[t][:].indirect(offs_t[:, s * (CUT // 16) : (s + 1) * (CUT // 16)])
+                )
+            g4s[s] = g4
+
+        def interleave_w(s):
+            wg = keep.tile([P, 2, N, PACK], BF16, name="wg%d" % s, align_bytes=64)
+            nc.scalar.copy(wg[:], w_raw[s][:].rearrange("p e j n -> p e n j"))
+            wgs[s] = wg
+
+        def interleave_x(s):
+            xg = keep.tile([P, CUT, PACK], BF16, name="xg%d" % s, align_bytes=64)
+            nc.scalar.copy(xg[:], g4s[s][:].rearrange("p t n -> p n t"))
+            xgs[s] = xg
+
+        def quantize(s):
+            cols = slice(s * CUT, (s + 1) * CUT)
+            nc.vector.quantize_mx(
+                out=w_codes[:, cols].bitcast(FP8X4),
+                scales=w_scales[:, cols],
+                in_=wgs[s][:].rearrange("p e n j -> p (e n j)"),
+            )
+            nc.vector.quantize_mx(
+                out=x_codes[:, cols].bitcast(FP8X4),
+                scales=x_scales[:, cols],
+                in_=xgs[s][:].rearrange("p n t -> p (n t)"),
+            )
+
+        def multiply(s):
+            acc = psum.tile([P, CUT], F32, name="acc%d" % s)
+            for h in range(CUT // C):
+                e = s * (CUT // C) + h
+                cols = slice(e * C, (e + 1) * C)
+                nc.tensor.matmul_mx(
+                    out=acc[:, h * C : (h + 1) * C],
+                    lhsT=w_codes[:, cols].bitcast(FP8X4),
+                    lhsT_scale=w_scales[:, cols],
+                    rhs=x_codes[:, cols].bitcast(FP8X4),
+                    rhs_scale=x_scales[:, cols],
+                    start=True,
+                    stop=True,
+                )
+            nc.scalar.copy(y[:, s * CUT : (s + 1) * CUT], acc[:])
+
+        gather(0)
+        interleave_w(0)
+        interleave_x(0)
+        for s in range(1, N_CUTS):
+            gather(s)
+            interleave_w(s)
+            interleave_x(s)
+            quantize(s - 1)
+            multiply(s - 1)
+        quantize(N_CUTS - 1)
+        multiply(N_CUTS - 1)
+
+        for h in range(2):
+            tok = slice(h * HALF, (h + 1) * HALF)
+            lst = slice(h * (HALF // 16), (h + 1) * (HALF // 16))
+            first = keep.tile([P, HALF], F32, name="first%d" % h)
+            second = keep.tile([P, HALF], F32, name="second%d" % h)
+            total = keep.tile([P, HALF], F32, name="total%d" % h)
+            nc.vector.tensor_tensor(first[:], y[:].indirect(pos1_t[:, lst]), gates[0][:, tok], MULT)
+            nc.vector.tensor_tensor(second[:], y[:].indirect(pos2_t[:, lst]), gates[1][:, tok], MULT)
+            nc.vector.tensor_tensor(total[:], first[:], second[:], ADD)
+            nc.sync.dma_start(out[:, tok], total[:])

@@ -18,7 +18,7 @@ P = 128
 PACK = 4
 SLOTS = E * C
 CUT = 256
-N_CUTS = SLOTS // CUT
+GATHERS = ((0, 352), (352, 704), (704, 1024))
 HALF = T // 2
 
 
@@ -33,11 +33,6 @@ def tile_routed_moe_kernel(tc, xT, w, gate, offs, pos1, pos2, out):
         pos1_t = lists.tile([P, T // 16], U16, name="pos1_t")
         pos2_t = lists.tile([P, T // 16], U16, name="pos2_t")
 
-        warm_in = keep.tile([P, 1], F32, name="warm_in")
-        warm_out = keep.tile([P, 1], F32, name="warm_out")
-        nc.vector.memset(warm_in[:], 0.0)
-        nc.scalar.copy(warm_out[:], warm_in[:])
-
         nc.sync.dma_start(offs_t[:], offs)
         planes = xT.rearrange("(p t) n -> p t n", t=PACK)
         xp = []
@@ -46,8 +41,9 @@ def tile_routed_moe_kernel(tc, xT, w, gate, offs, pos1, pos2, out):
             nc.sync.dma_start(plane[:], planes[:, t, :])
             xp.append(plane)
         w_raw = []
-        for c in range(N_CUTS):
-            raw = keep.tile([P, 2, PACK, N], F32, name="w_raw%d" % c)
+        for c in range(4):
+            tag = "turn" if c == 3 else "w_raw%d" % c
+            raw = keep.tile([P, 2, PACK, N], F32, name="w_raw%d" % c, tag=tag, align_bytes=64)
             nc.sync.dma_start(
                 raw[:].rearrange("p e j n -> p e (j n)"),
                 w[2 * c : 2 * c + 2].rearrange("e (p j) n -> p e (j n)", j=PACK),
@@ -61,80 +57,65 @@ def tile_routed_moe_kernel(tc, xT, w, gate, offs, pos1, pos2, out):
             nc.sync.dma_start(g[:], gate[r])
             gates.append(g)
 
+        y = keep.tile([P, SLOTS], F32, name="y")
+        wg = keep.tile([P, E, N, PACK], BF16, name="wg", align_bytes=64)
         w_codes = keep.tile([P, SLOTS], U32, name="w_codes", align_bytes=64)
         w_scales = keep.tile([P, SLOTS], U8, name="w_scales", align_bytes=64)
-        x_codes = keep.tile([P, SLOTS], U32, name="x_codes", align_bytes=64)
-        x_scales = keep.tile([P, SLOTS], U8, name="x_scales", align_bytes=64)
-        y = keep.tile([P, SLOTS], F32, name="y")
 
-        g4s, xgs, wgs = {}, {}, {}
+        for c in range(4):
+            nc.scalar.copy(wg[:, 2 * c : 2 * c + 2], w_raw[c][:].rearrange("p e j n -> p e n j"))
 
-        def gather(s):
-            g4 = keep.tile([P, PACK, CUT], F32, name="g4_%d" % s)
+        g4 = keep.tile([P, PACK, SLOTS], F32, name="g4")
+        for a, b in GATHERS:
             for t in range(PACK):
-                nc.vector.tensor_copy(
-                    g4[:, t, :], xp[t][:].indirect(offs_t[:, s * (CUT // 16) : (s + 1) * (CUT // 16)])
-                )
-            g4s[s] = g4
+                nc.vector.tensor_copy(g4[:, t, a:b], xp[t][:].indirect(offs_t[:, a // 16 : b // 16]))
 
-        def interleave_w(s):
-            wg = keep.tile([P, 2, N, PACK], BF16, name="wg%d" % s, align_bytes=64)
-            nc.scalar.copy(wg[:], w_raw[s][:].rearrange("p e j n -> p e n j"))
-            wgs[s] = wg
-
-        def interleave_x(s):
-            xg = keep.tile([P, CUT, PACK], BF16, name="xg%d" % s, align_bytes=64)
-            nc.scalar.copy(xg[:], g4s[s][:].rearrange("p t n -> p n t"))
-            xgs[s] = xg
-
-        def quantize(s):
+        xg_s = keep.tile([P, 3 * CUT, PACK], BF16, name="xg_s", tag="turn", align_bytes=64)
+        xg_v = keep.tile([P, CUT, PACK], BF16, name="xg_v", align_bytes=64)
+        for s in range(3):
             cols = slice(s * CUT, (s + 1) * CUT)
-            nc.vector.quantize_mx(
-                out=w_codes[:, cols].bitcast(FP8X4),
-                scales=w_scales[:, cols],
-                in_=wgs[s][:].rearrange("p e n j -> p (e n j)"),
-            )
-            nc.vector.quantize_mx(
-                out=x_codes[:, cols].bitcast(FP8X4),
-                scales=x_scales[:, cols],
-                in_=xgs[s][:].rearrange("p n t -> p (n t)"),
-            )
+            nc.scalar.copy(xg_s[:, cols, :], g4[:, :, cols].rearrange("p t n -> p n t"))
+        nc.vector.tensor_copy(xg_v[:], g4[:, :, 3 * CUT : 4 * CUT].rearrange("p t n -> p n t"))
 
-        def multiply(s):
-            acc = psum.tile([P, CUT], F32, name="acc%d" % s)
-            for h in range(CUT // C):
-                e = s * (CUT // C) + h
-                cols = slice(e * C, (e + 1) * C)
+        nc.vector.quantize_mx(
+            out=w_codes[:].bitcast(FP8X4), scales=w_scales[:], in_=wg[:].rearrange("p e n j -> p (e n j)")
+        )
+
+        def tokens(grouped, first_slot, n_slots, name, leave_on_vector):
+            codes = keep.tile([P, n_slots], U32, name="x_codes" + name, align_bytes=64)
+            scales = keep.tile([P, n_slots], U8, name="x_scales" + name, align_bytes=64)
+            nc.vector.quantize_mx(
+                out=codes[:].bitcast(FP8X4), scales=scales[:], in_=grouped.rearrange("p n t -> p (n t)")
+            )
+            acc = psum.tile([P, n_slots], F32, name="acc" + name)
+            for h in range(n_slots // C):
+                cols = slice(h * C, (h + 1) * C)
+                wcols = slice(first_slot + h * C, first_slot + (h + 1) * C)
                 nc.tensor.matmul_mx(
-                    out=acc[:, h * C : (h + 1) * C],
-                    lhsT=w_codes[:, cols].bitcast(FP8X4),
-                    lhsT_scale=w_scales[:, cols],
-                    rhs=x_codes[:, cols].bitcast(FP8X4),
-                    rhs_scale=x_scales[:, cols],
+                    out=acc[:, cols],
+                    lhsT=w_codes[:, wcols].bitcast(FP8X4),
+                    lhsT_scale=w_scales[:, wcols],
+                    rhs=codes[:, cols].bitcast(FP8X4),
+                    rhs_scale=scales[:, cols],
                     start=True,
                     stop=True,
                 )
-            nc.scalar.copy(y[:, s * CUT : (s + 1) * CUT], acc[:])
+            if leave_on_vector:
+                nc.vector.tensor_copy(y[:, first_slot : first_slot + n_slots], acc[:])
+            else:
+                nc.scalar.copy(y[:, first_slot : first_slot + n_slots], acc[:])
 
-        gather(0)
-        interleave_w(0)
-        interleave_x(0)
-        for s in range(1, N_CUTS):
-            gather(s)
-            interleave_w(s)
-            interleave_x(s)
-            quantize(s - 1)
-            multiply(s - 1)
-        quantize(N_CUTS - 1)
-        multiply(N_CUTS - 1)
+        tokens(xg_v[:], 3 * CUT, CUT, "3", False)
+        tokens(xg_s[:, 0:CUT, :], 0, CUT, "0", False)
+        tokens(xg_s[:, CUT : 2 * CUT, :], CUT, CUT, "1", True)
+        tokens(xg_s[:, 2 * CUT : 3 * CUT, :], 2 * CUT, CUT, "2", True)
 
+        first = keep.tile([P, T], F32, name="first")
+        second = keep.tile([P, T], F32, name="second")
+        total = keep.tile([P, T], F32, name="total")
+        nc.vector.tensor_tensor(first[:], y[:].indirect(pos1_t[:]), gates[0][:], MULT)
+        nc.vector.tensor_tensor(second[:], y[:].indirect(pos2_t[:]), gates[1][:], MULT)
         for h in range(2):
             tok = slice(h * HALF, (h + 1) * HALF)
-            lst = slice(h * (HALF // 16), (h + 1) * (HALF // 16))
-            first = keep.tile([P, HALF], F32, name="first%d" % h)
-            second = keep.tile([P, HALF], F32, name="second%d" % h)
-            total = keep.tile([P, HALF], F32, name="total%d" % h)
-            nc.vector.tensor_tensor(first[:], y[:].indirect(pos1_t[:, lst]), gates[0][:, tok], MULT)
-            nc.vector.tensor_tensor(second[:], y[:].indirect(pos2_t[:, lst]), gates[1][:, tok], MULT)
-            nc.vector.tensor_tensor(total[:], first[:], second[:], ADD)
-            nc.sync.dma_start(out[:, tok], total[:])
+            nc.vector.tensor_tensor(total[:, tok], first[:, tok], second[:, tok], ADD)
+            nc.sync.dma_start(out[:, tok], total[:, tok])

@@ -58,7 +58,7 @@ def tile_routed_moe_kernel(tc, xT, w, gate, offs, pos1, pos2, out):
             gates.append(g)
 
         y = keep.tile([P, SLOTS], F32, name="y")
-        wg = keep.tile([P, E, N, PACK], BF16, name="wg", align_bytes=64)
+        wg = keep.tile([P, E, N, PACK], BF16, name="wg", tag="turn_v", align_bytes=64)
         w_codes = keep.tile([P, SLOTS], U32, name="w_codes", align_bytes=64)
         w_scales = keep.tile([P, SLOTS], U8, name="w_scales", align_bytes=64)
 
@@ -70,16 +70,16 @@ def tile_routed_moe_kernel(tc, xT, w, gate, offs, pos1, pos2, out):
             for t in range(PACK):
                 nc.vector.tensor_copy(g4[:, t, a:b], xp[t][:].indirect(offs_t[:, a // 16 : b // 16]))
 
+        nc.vector.quantize_mx(
+            out=w_codes[:].bitcast(FP8X4), scales=w_scales[:], in_=wg[:].rearrange("p e n j -> p (e n j)")
+        )
+
         xg_s = keep.tile([P, 3 * CUT, PACK], BF16, name="xg_s", tag="turn", align_bytes=64)
-        xg_v = keep.tile([P, CUT, PACK], BF16, name="xg_v", align_bytes=64)
+        xg_v = keep.tile([P, CUT, PACK], BF16, name="xg_v", tag="turn_v", align_bytes=64)
         for s in range(3):
             cols = slice(s * CUT, (s + 1) * CUT)
             nc.scalar.copy(xg_s[:, cols, :], g4[:, :, cols].rearrange("p t n -> p n t"))
         nc.vector.tensor_copy(xg_v[:], g4[:, :, 3 * CUT : 4 * CUT].rearrange("p t n -> p n t"))
-
-        nc.vector.quantize_mx(
-            out=w_codes[:].bitcast(FP8X4), scales=w_scales[:], in_=wg[:].rearrange("p e n j -> p (e n j)")
-        )
 
         def tokens(grouped, first_slot, n_slots, name, leave_on_vector):
             codes = keep.tile([P, n_slots], U32, name="x_codes" + name, align_bytes=64)
@@ -107,7 +107,7 @@ def tile_routed_moe_kernel(tc, xT, w, gate, offs, pos1, pos2, out):
 
         tokens(xg_v[:], 3 * CUT, CUT, "3", False)
         tokens(xg_s[:, 0:CUT, :], 0, CUT, "0", False)
-        tokens(xg_s[:, CUT : 2 * CUT, :], CUT, CUT, "1", True)
+        tokens(xg_s[:, CUT : 2 * CUT, :], CUT, CUT, "1", False)
         tokens(xg_s[:, 2 * CUT : 3 * CUT, :], 2 * CUT, CUT, "2", True)
 
         first = keep.tile([P, T], F32, name="first")

@@ -63,7 +63,10 @@ def tile_routed_moe_kernel(tc, xT, w, gate, offs, pos1, pos2, out):
         w_scales = keep.tile([P, SLOTS], U8, name="w_scales", align_bytes=64)
 
         for c in range(4):
-            nc.scalar.copy(wg[:, 2 * c : 2 * c + 2], w_raw[c][:].rearrange("p e j n -> p e n j"))
+            nc.scalar.copy(
+                wg[:, 2 * c : 2 * c + 2].rearrange("p e (c i) j -> p e c j i", i=4),
+                w_raw[c][:].rearrange("p e j (c i) -> p e c j i", i=4),
+            )
 
         g4 = keep.tile([P, PACK, SLOTS], F32, name="g4")
         for a, b in GATHERS:
@@ -78,8 +81,14 @@ def tile_routed_moe_kernel(tc, xT, w, gate, offs, pos1, pos2, out):
         xg_v = keep.tile([P, CUT, PACK], BF16, name="xg_v", tag="turn_v", align_bytes=64)
         for s in range(3):
             cols = slice(s * CUT, (s + 1) * CUT)
-            nc.scalar.copy(xg_s[:, cols, :], g4[:, :, cols].rearrange("p t n -> p n t"))
-        nc.vector.tensor_copy(xg_v[:], g4[:, :, 3 * CUT : 4 * CUT].rearrange("p t n -> p n t"))
+            nc.scalar.copy(
+                xg_s[:, cols, :].rearrange("p (c i) t -> p c t i", i=4),
+                g4[:, :, cols].rearrange("p t (c i) -> p c t i", i=4),
+            )
+        nc.vector.tensor_copy(
+            xg_v[:].rearrange("p (c i) t -> p c t i", i=4),
+            g4[:, :, 3 * CUT : 4 * CUT].rearrange("p t (c i) -> p c t i", i=4),
+        )
 
         def tokens(grouped, first_slot, n_slots, name, leave_on_vector):
             codes = keep.tile([P, n_slots], U32, name="x_codes" + name, align_bytes=64)

@@ -114,16 +114,20 @@ def tile_routed_moe_kernel(tc, xT, w, gate, offs, pos1, pos2, out):
             else:
                 nc.scalar.copy(y[:, first_slot : first_slot + n_slots], acc[:])
 
-        tokens(xg_v[:], 3 * CUT, CUT, "3", False)
         tokens(xg_s[:, 0:CUT, :], 0, CUT, "0", False)
         tokens(xg_s[:, CUT : 2 * CUT, :], CUT, CUT, "1", False)
-        tokens(xg_s[:, 2 * CUT : 3 * CUT, :], 2 * CUT, CUT, "2", True)
+        tokens(xg_v[:], 3 * CUT, CUT, "3", False)
+        tokens(xg_s[:, 2 * CUT : 2 * CUT + C, :], 2 * CUT, C, "2a", False)
+        tokens(xg_s[:, 2 * CUT + C : 3 * CUT, :], 2 * CUT + C, C, "2b", True)
 
         first = keep.tile([P, T], F32, name="first")
         second = keep.tile([P, T], F32, name="second")
         total = keep.tile([P, T], F32, name="total")
         nc.vector.tensor_tensor(first[:], y[:].indirect(pos1_t[:]), gates[0][:], MULT)
-        nc.vector.tensor_tensor(second[:], y[:].indirect(pos2_t[:]), gates[1][:], MULT)
+        for h in range(2):
+            tok = slice(h * HALF, (h + 1) * HALF)
+            lst = slice(h * (HALF // 16), (h + 1) * (HALF // 16))
+            nc.vector.tensor_tensor(second[:, tok], y[:].indirect(pos2_t[:, lst]), gates[1][:, tok], MULT)
         for h in range(2):
             tok = slice(h * HALF, (h + 1) * HALF)
             nc.vector.tensor_tensor(total[:, tok], first[:, tok], second[:, tok], ADD)

@@ -13,6 +13,7 @@ U8 = mybir.dt.uint8
 FP8X4 = mybir.dt.float8_e4m3fn_x4
 MULT = mybir.AluOpType.mult
 ADD = mybir.AluOpType.add
+COPY = mybir.ActivationFunctionType.Copy
 
 P = 128
 PACK = 4
@@ -35,15 +36,14 @@ def tile_routed_moe_kernel(tc, xT, w, gate, offs, pos1, pos2, out):
 
         nc.sync.dma_start(offs_t[:], offs)
         planes = xT.rearrange("(p t) n -> p t n", t=PACK)
-        xp = []
-        for t in range(PACK):
+        xp = {}
+        for t in (0, 2, 1, 3):
             plane = keep.tile([P, T], F32, name="xp%d" % t)
             nc.sync.dma_start(plane[:], planes[:, t, :])
-            xp.append(plane)
+            xp[t] = plane
         w_raw = []
         for c in range(4):
-            tag = "turn" if c == 3 else "w_raw%d" % c
-            raw = keep.tile([P, 2, PACK, N], F32, name="w_raw%d" % c, tag=tag, align_bytes=64)
+            raw = keep.tile([P, 2, PACK, N], F32, name="w_raw%d" % c, tag="turn" if c == 2 else "w_raw%d" % c, align_bytes=64)
             nc.sync.dma_start(
                 raw[:].rearrange("p e j n -> p e (j n)"),
                 w[2 * c : 2 * c + 2].rearrange("e (p j) n -> p e (j n)", j=PACK),
@@ -58,43 +58,60 @@ def tile_routed_moe_kernel(tc, xT, w, gate, offs, pos1, pos2, out):
             gates.append(g)
 
         y = keep.tile([P, SLOTS], F32, name="y")
-        wg = keep.tile([P, E, N, PACK], BF16, name="wg", tag="turn_v", align_bytes=64)
+        wg = keep.tile([P, E, N, PACK], BF16, name="wg", align_bytes=64)
         w_codes = keep.tile([P, SLOTS], U32, name="w_codes", align_bytes=64)
         w_scales = keep.tile([P, SLOTS], U8, name="w_scales", align_bytes=64)
+        xb = keep.tile([P, 2, T], BF16, name="xb", align_bytes=64)
+        xg = keep.tile([P, SLOTS, PACK], BF16, name="xg", align_bytes=64)
+        g2 = keep.tile([P, 2, SLOTS], F32, name="g2")
 
-        for c in range(4):
-            nc.scalar.copy(
+        for u in range(2):
+            nc.scalar.copy(xb[:, u, :], xp[2 + u][:])
+        for t in range(2):
+            for a, b in GATHERS:
+                nc.vector.tensor_copy(g2[:, t, a:b], xp[t][:].indirect(offs_t[:, a // 16 : b // 16]))
+        for u in range(2):
+            for e in range(E):
+                nc.scalar.activation(
+                    xg[:, e * C : (e + 1) * C, 2 + u], xb[:, u, :].indirect(offs_t[:, e * (C // 16) : (e + 1) * (C // 16)]), COPY
+                )
+
+        def cast_w(engine_copy, c):
+            engine_copy(
                 wg[:, 2 * c : 2 * c + 2].rearrange("p e (c i) j -> p e c j i", i=4),
                 w_raw[c][:].rearrange("p e j (c i) -> p e c j i", i=4),
             )
 
-        g4 = keep.tile([P, PACK, SLOTS], F32, name="g4")
-        for a, b in GATHERS:
-            for t in range(PACK):
-                nc.vector.tensor_copy(g4[:, t, a:b], xp[t][:].indirect(offs_t[:, a // 16 : b // 16]))
-
-        nc.vector.quantize_mx(
-            out=w_codes[:].bitcast(FP8X4), scales=w_scales[:], in_=wg[:].rearrange("p e n j -> p (e n j)")
-        )
-
-        xg_s = keep.tile([P, 3 * CUT, PACK], BF16, name="xg_s", tag="turn", align_bytes=64)
-        xg_v = keep.tile([P, CUT, PACK], BF16, name="xg_v", tag="turn_v", align_bytes=64)
-        for s in range(3):
-            cols = slice(s * CUT, (s + 1) * CUT)
-            nc.scalar.copy(
-                xg_s[:, cols, :].rearrange("p (c i) t -> p c t i", i=4),
-                g4[:, :, cols].rearrange("p t (c i) -> p c t i", i=4),
+        def quantize_w(c0, c1):
+            cols = slice(c0 * 2 * C, c1 * 2 * C)
+            nc.vector.quantize_mx(
+                out=w_codes[:, cols].bitcast(FP8X4),
+                scales=w_scales[:, cols],
+                in_=wg[:, 2 * c0 : 2 * c1].rearrange("p e n j -> p (e n j)"),
             )
-        nc.vector.tensor_copy(
-            xg_v[:].rearrange("p (c i) t -> p c t i", i=4),
-            g4[:, :, 3 * CUT : 4 * CUT].rearrange("p t (c i) -> p c t i", i=4),
-        )
 
-        def tokens(grouped, first_slot, n_slots, name, leave_on_vector):
-            codes = keep.tile([P, n_slots], U32, name="x_codes" + name, align_bytes=64)
+        for c in range(3):
+            cast_w(nc.vector.tensor_copy, c)
+        cast_w(nc.scalar.copy, 3)
+
+        for s in range(4):
+            cols = slice(s * CUT, (s + 1) * CUT)
+            nc.vector.tensor_copy(
+                xg[:, cols, 0:2].rearrange("p (c i) t -> p c t i", i=4),
+                g2[:, :, cols].rearrange("p t (c i) -> p c t i", i=4),
+            )
+
+        quantize_w(0, 2)
+        quantize_w(2, 3)
+        quantize_w(3, 4)
+
+        def tokens(first_slot, n_slots, name, leave_on_vector):
+            codes = keep.tile([P, n_slots], U32, name="x_codes" + name, tag="turn" if first_slot == 0 else "x_codes" + name, align_bytes=64)
             scales = keep.tile([P, n_slots], U8, name="x_scales" + name, align_bytes=64)
             nc.vector.quantize_mx(
-                out=codes[:].bitcast(FP8X4), scales=scales[:], in_=grouped.rearrange("p n t -> p (n t)")
+                out=codes[:].bitcast(FP8X4),
+                scales=scales[:],
+                in_=xg[:, first_slot : first_slot + n_slots, :].rearrange("p n t -> p (n t)"),
             )
             acc = psum.tile([P, n_slots], F32, name="acc" + name)
             for h in range(n_slots // C):
@@ -114,11 +131,11 @@ def tile_routed_moe_kernel(tc, xT, w, gate, offs, pos1, pos2, out):
             else:
                 nc.scalar.copy(y[:, first_slot : first_slot + n_slots], acc[:])
 
-        tokens(xg_s[:, 0:CUT, :], 0, CUT, "0", False)
-        tokens(xg_s[:, CUT : 2 * CUT, :], CUT, CUT, "1", False)
-        tokens(xg_v[:], 3 * CUT, CUT, "3", False)
-        tokens(xg_s[:, 2 * CUT : 2 * CUT + C, :], 2 * CUT, C, "2a", False)
-        tokens(xg_s[:, 2 * CUT + C : 3 * CUT, :], 2 * CUT + C, C, "2b", True)
+        tokens(0, CUT, "0", False)
+        tokens(CUT, CUT, "1", False)
+        tokens(2 * CUT, CUT, "2", False)
+        tokens(3 * CUT, C, "3a", False)
+        tokens(3 * CUT + C, C, "3b", True)
 
         first = keep.tile([P, T], F32, name="first")
         second = keep.tile([P, T], F32, name="second")

@@ -43,7 +43,7 @@ def tile_routed_moe_kernel(tc, xT, w, gate, offs, pos1, pos2, out):
             xp[t] = plane
         w_raw = []
         for c in range(4):
-            raw = keep.tile([P, 2, PACK, N], F32, name="w_raw%d" % c, tag="turn" if c == 2 else "w_raw%d" % c, align_bytes=64)
+            raw = keep.tile([P, 2, PACK, N], F32, name="w_raw%d" % c, tag="turn_b" if c == 2 else "w_raw%d" % c, align_bytes=64)
             nc.sync.dma_start(
                 raw[:].rearrange("p e j n -> p e (j n)"),
                 w[2 * c : 2 * c + 2].rearrange("e (p j) n -> p e (j n)", j=PACK),
@@ -58,8 +58,8 @@ def tile_routed_moe_kernel(tc, xT, w, gate, offs, pos1, pos2, out):
             gates.append(g)
 
         y = keep.tile([P, SLOTS], F32, name="y")
-        wg = keep.tile([P, E, N, PACK], BF16, name="wg", align_bytes=64)
-        w_codes = keep.tile([P, SLOTS], U32, name="w_codes", align_bytes=64)
+        wg_v = keep.tile([P, 6, N, PACK], BF16, name="wg_v", tag="turn_g", align_bytes=64)
+        wg_s = keep.tile([P, 2, N, PACK], BF16, name="wg_s", align_bytes=64)
         w_scales = keep.tile([P, SLOTS], U8, name="w_scales", align_bytes=64)
         xb = keep.tile([P, 2, T], BF16, name="xb", align_bytes=64)
         xg = keep.tile([P, SLOTS, PACK], BF16, name="xg", align_bytes=64)
@@ -76,23 +76,23 @@ def tile_routed_moe_kernel(tc, xT, w, gate, offs, pos1, pos2, out):
                     xg[:, e * C : (e + 1) * C, 2 + u], xb[:, u, :].indirect(offs_t[:, e * (C // 16) : (e + 1) * (C // 16)]), COPY
                 )
 
-        def cast_w(engine_copy, c):
+        def cast_w(engine_copy, grouped, c):
             engine_copy(
-                wg[:, 2 * c : 2 * c + 2].rearrange("p e (c i) j -> p e c j i", i=4),
+                grouped.rearrange("p e (c i) j -> p e c j i", i=4),
                 w_raw[c][:].rearrange("p e j (c i) -> p e c j i", i=4),
             )
 
-        def quantize_w(c0, c1):
+        def quantize_w(grouped, c0, c1):
             cols = slice(c0 * 2 * C, c1 * 2 * C)
             nc.vector.quantize_mx(
                 out=w_codes[:, cols].bitcast(FP8X4),
                 scales=w_scales[:, cols],
-                in_=wg[:, 2 * c0 : 2 * c1].rearrange("p e n j -> p (e n j)"),
+                in_=grouped.rearrange("p e n j -> p (e n j)"),
             )
 
         for c in range(3):
-            cast_w(nc.vector.tensor_copy, c)
-        cast_w(nc.scalar.copy, 3)
+            cast_w(nc.vector.tensor_copy, wg_v[:, 2 * c : 2 * c + 2], c)
+        cast_w(nc.scalar.copy, wg_s[:], 3)
 
         for s in range(4):
             cols = slice(s * CUT, (s + 1) * CUT)
@@ -101,41 +101,39 @@ def tile_routed_moe_kernel(tc, xT, w, gate, offs, pos1, pos2, out):
                 g2[:, :, cols].rearrange("p t (c i) -> p c t i", i=4),
             )
 
-        quantize_w(0, 2)
-        quantize_w(2, 3)
-        quantize_w(3, 4)
+        w_codes = keep.tile([P, SLOTS], U32, name="w_codes", tag="turn_b", align_bytes=64)
+        quantize_w(wg_v[:, 0:4], 0, 2)
+        quantize_w(wg_v[:, 4:6], 2, 3)
+        x_codes = keep.tile([P, SLOTS], U32, name="x_codes", tag="turn_g", align_bytes=64)
+        x_scales = keep.tile([P, SLOTS], U8, name="x_scales", align_bytes=64)
 
-        def tokens(first_slot, n_slots, name, leave_on_vector):
-            codes = keep.tile([P, n_slots], U32, name="x_codes" + name, tag="turn" if first_slot == 0 else "x_codes" + name, align_bytes=64)
-            scales = keep.tile([P, n_slots], U8, name="x_scales" + name, align_bytes=64)
+        def tokens(first_slot, n_slots):
+            piece = slice(first_slot, first_slot + n_slots)
             nc.vector.quantize_mx(
-                out=codes[:].bitcast(FP8X4),
-                scales=scales[:],
-                in_=xg[:, first_slot : first_slot + n_slots, :].rearrange("p n t -> p (n t)"),
+                out=x_codes[:, piece].bitcast(FP8X4),
+                scales=x_scales[:, piece],
+                in_=xg[:, piece, :].rearrange("p n t -> p (n t)"),
             )
-            acc = psum.tile([P, n_slots], F32, name="acc" + name)
+            acc = psum.tile([P, n_slots], F32, name="acc%d" % first_slot)
             for h in range(n_slots // C):
-                cols = slice(h * C, (h + 1) * C)
-                wcols = slice(first_slot + h * C, first_slot + (h + 1) * C)
+                cols = slice(first_slot + h * C, first_slot + (h + 1) * C)
                 nc.tensor.matmul_mx(
-                    out=acc[:, cols],
-                    lhsT=w_codes[:, wcols].bitcast(FP8X4),
-                    lhsT_scale=w_scales[:, wcols],
-                    rhs=codes[:, cols].bitcast(FP8X4),
-                    rhs_scale=scales[:, cols],
+                    out=acc[:, h * C : (h + 1) * C],
+                    lhsT=w_codes[:, cols].bitcast(FP8X4),
+                    lhsT_scale=w_scales[:, cols],
+                    rhs=x_codes[:, cols].bitcast(FP8X4),
+                    rhs_scale=x_scales[:, cols],
                     start=True,
                     stop=True,
                 )
-            if leave_on_vector:
-                nc.vector.tensor_copy(y[:, first_slot : first_slot + n_slots], acc[:])
-            else:
-                nc.scalar.copy(y[:, first_slot : first_slot + n_slots], acc[:])
+            nc.scalar.copy(y[:, piece], acc[:])
 
-        tokens(0, CUT, "0", False)
-        tokens(CUT, CUT, "1", False)
-        tokens(2 * CUT, CUT, "2", False)
-        tokens(3 * CUT, C, "3a", False)
-        tokens(3 * CUT + C, C, "3b", True)
+        tokens(0, CUT)
+        tokens(CUT, CUT)
+        tokens(2 * CUT, CUT)
+        quantize_w(wg_s[:], 3, 4)
+        tokens(3 * CUT, C)
+        tokens(3 * CUT + C, C)
 
         first = keep.tile([P, T], F32, name="first")
         second = keep.tile([P, T], F32, name="second")

@@ -19,7 +19,7 @@ P = 128
 PACK = 4
 SLOTS = E * C
 CUT = 256
-GATHERS = ((0, 352), (352, 704), (704, 1024))
+GATHERS = ((0, 512), (512, 1024))
 HALF = T // 2
 
 
@@ -38,17 +38,20 @@ def tile_routed_moe_kernel(tc, xT, w, gate, offs, pos1, pos2, out):
         planes = xT.rearrange("(p t) n -> p t n", t=PACK)
         xp = {}
         for t in (0, 2, 1, 3):
-            plane = keep.tile([P, T], F32, name="xp%d" % t)
-            nc.sync.dma_start(plane[:], planes[:, t, :])
+            plane = keep.tile([P, 2 * T if t < 2 else T], F32, name="xp%d" % t)
+            nc.sync.dma_start(plane[:, 0:T], planes[:, t, :])
             xp[t] = plane
-        w_raw = []
-        for c in range(4):
-            raw = keep.tile([P, 2, PACK, N], F32, name="w_raw%d" % c, tag="turn_b" if c == 2 else "w_raw%d" % c, align_bytes=64)
+
+        def load_w(e0, e1, name):
+            raw = keep.tile([P, e1 - e0, PACK, N], F32, name=name, tag=name, align_bytes=64)
             nc.sync.dma_start(
                 raw[:].rearrange("p e j n -> p e (j n)"),
-                w[2 * c : 2 * c + 2].rearrange("e (p j) n -> p e (j n)", j=PACK),
+                w[e0:e1].rearrange("e (p j) n -> p e (j n)", j=PACK),
             )
-            w_raw.append(raw)
+            return raw
+
+        w_raw_v = load_w(0, 6, "turn_w")
+        w_raw_s = load_w(6, 8, "w_raw_s")
         nc.sync.dma_start(pos1_t[:], pos1)
         nc.sync.dma_start(pos2_t[:], pos2)
         gates = []
@@ -58,7 +61,7 @@ def tile_routed_moe_kernel(tc, xT, w, gate, offs, pos1, pos2, out):
             gates.append(g)
 
         y = keep.tile([P, SLOTS], F32, name="y")
-        wg_v = keep.tile([P, 6, N, PACK], BF16, name="wg_v", tag="turn_g", align_bytes=64)
+        wg_v = keep.tile([P, 6, N, PACK], BF16, name="wg_v", align_bytes=64)
         wg_s = keep.tile([P, 2, N, PACK], BF16, name="wg_s", align_bytes=64)
         w_scales = keep.tile([P, SLOTS], U8, name="w_scales", align_bytes=64)
         xb = keep.tile([P, 2, T], BF16, name="xb", align_bytes=64)
@@ -76,10 +79,10 @@ def tile_routed_moe_kernel(tc, xT, w, gate, offs, pos1, pos2, out):
                     xg[:, e * C : (e + 1) * C, 2 + u], xb[:, u, :].indirect(offs_t[:, e * (C // 16) : (e + 1) * (C // 16)]), COPY
                 )
 
-        def cast_w(engine_copy, grouped, c):
+        def cast_w(engine_copy, grouped, raw):
             engine_copy(
                 grouped.rearrange("p e (c i) j -> p e c j i", i=4),
-                w_raw[c][:].rearrange("p e j (c i) -> p e c j i", i=4),
+                raw.rearrange("p e j (c i) -> p e c j i", i=4),
             )
 
         def quantize_w(grouped, c0, c1):
@@ -90,21 +93,21 @@ def tile_routed_moe_kernel(tc, xT, w, gate, offs, pos1, pos2, out):
                 in_=grouped.rearrange("p e n j -> p (e n j)"),
             )
 
-        for c in range(3):
-            cast_w(nc.vector.tensor_copy, wg_v[:, 2 * c : 2 * c + 2], c)
-        cast_w(nc.scalar.copy, wg_s[:], 3)
+        cast_w(nc.vector.tensor_copy, wg_v[:, 0:4], w_raw_v[:, 0:4])
+        cast_w(nc.vector.tensor_copy, wg_v[:, 4:6], w_raw_v[:, 4:6])
+        cast_w(nc.scalar.copy, wg_s[:], w_raw_s[:])
 
-        for s in range(4):
-            cols = slice(s * CUT, (s + 1) * CUT)
+        for s in range(2):
+            cols = slice(s * 2 * CUT, (s + 1) * 2 * CUT)
             nc.vector.tensor_copy(
                 xg[:, cols, 0:2].rearrange("p (c i) t -> p c t i", i=4),
                 g2[:, :, cols].rearrange("p t (c i) -> p c t i", i=4),
             )
 
-        w_codes = keep.tile([P, SLOTS], U32, name="w_codes", tag="turn_b", align_bytes=64)
+        w_codes = keep.tile([P, SLOTS], U32, name="w_codes", align_bytes=64)
         quantize_w(wg_v[:, 0:4], 0, 2)
         quantize_w(wg_v[:, 4:6], 2, 3)
-        x_codes = keep.tile([P, SLOTS], U32, name="x_codes", tag="turn_g", align_bytes=64)
+        x_codes = keep.tile([P, SLOTS], U32, name="x_codes", tag="turn_w", align_bytes=64)
         x_scales = keep.tile([P, SLOTS], U8, name="x_scales", align_bytes=64)
 
         def tokens(first_slot, n_slots):

@@ -37,7 +37,8 @@ def tile_routed_moe_kernel(tc, xT, w, gate, offs, pos1, pos2, out):
         nc.sync.dma_start(offs_t[:], offs)
         planes = xT.rearrange("(p t) n -> p t n", t=PACK)
         xp = {}
-        for t in (0, 2, 1, 3):
+
+        def load_plane(t):
             plane = keep.tile([P, 2 * T if t < 2 else T], F32, name="xp%d" % t)
             nc.sync.dma_start(plane[:, 0:T], planes[:, t, :])
             xp[t] = plane
@@ -50,8 +51,13 @@ def tile_routed_moe_kernel(tc, xT, w, gate, offs, pos1, pos2, out):
             )
             return raw
 
+        load_plane(0)
+        load_plane(2)
+        load_plane(1)
+        w_raw_g = load_w(7, 8, "w_raw_g")
+        load_plane(3)
         w_raw_v = load_w(0, 6, "turn_w")
-        w_raw_s = load_w(6, 8, "w_raw_s")
+        w_raw_s = load_w(6, 7, "w_raw_s")
         nc.sync.dma_start(pos1_t[:], pos1)
         nc.sync.dma_start(pos2_t[:], pos2)
         gates = []
@@ -95,7 +101,8 @@ def tile_routed_moe_kernel(tc, xT, w, gate, offs, pos1, pos2, out):
 
         cast_w(nc.vector.tensor_copy, wg_v[:, 0:4], w_raw_v[:, 0:4])
         cast_w(nc.vector.tensor_copy, wg_v[:, 4:6], w_raw_v[:, 4:6])
-        cast_w(nc.scalar.copy, wg_s[:], w_raw_s[:])
+        cast_w(nc.scalar.copy, wg_s[:, 0:1], w_raw_s[:])
+        nc.gpsimd.tensor_copy(wg_s[:, 1], w_raw_g[:, 0].rearrange("p j n -> p n j"))
 
         for s in range(2):
             cols = slice(s * 2 * CUT, (s + 1) * 2 * CUT)

@@ -54,8 +54,8 @@ def tile_routed_moe_kernel(tc, xT, w, gate, offs, pos1, pos2, out):
         load_plane(0)
         load_plane(2)
         load_plane(1)
-        w_raw_g = load_w(7, 8, "w_raw_g")
         load_plane(3)
+        w_raw_g = load_w(7, 8, "w_raw_g")
         w_raw_v = load_w(0, 6, "turn_w")
         w_raw_s = load_w(6, 7, "w_raw_s")
         nc.sync.dma_start(pos1_t[:], pos1)

@@ -91,8 +91,8 @@ def tile_routed_moe_kernel(tc, xT, w, gate, offs, pos1, pos2, out):
                 raw.rearrange("p e j (c i) -> p e c j i", i=4),
             )
 
-        def quantize_w(grouped, c0, c1):
-            cols = slice(c0 * 2 * C, c1 * 2 * C)
+        def quantize_w(grouped, e0, e1):
+            cols = slice(e0 * C, e1 * C)
             nc.vector.quantize_mx(
                 out=w_codes[:, cols].bitcast(FP8X4),
                 scales=w_scales[:, cols],
@@ -112,18 +112,21 @@ def tile_routed_moe_kernel(tc, xT, w, gate, offs, pos1, pos2, out):
             )
 
         w_codes = keep.tile([P, SLOTS], U32, name="w_codes", align_bytes=64)
-        quantize_w(wg_v[:, 0:4], 0, 2)
-        quantize_w(wg_v[:, 4:6], 2, 3)
+        quantize_w(wg_v[:, 0:4], 0, 4)
+        quantize_w(wg_v[:, 4:6], 4, 6)
+        quantize_w(wg_s[:, 1:2], 7, 8)
         x_codes = keep.tile([P, SLOTS], U32, name="x_codes", tag="turn_w", align_bytes=64)
         x_scales = keep.tile([P, SLOTS], U8, name="x_scales", align_bytes=64)
 
-        def tokens(first_slot, n_slots):
+        def quantize_x(first_slot, n_slots):
             piece = slice(first_slot, first_slot + n_slots)
             nc.vector.quantize_mx(
                 out=x_codes[:, piece].bitcast(FP8X4),
                 scales=x_scales[:, piece],
                 in_=xg[:, piece, :].rearrange("p n t -> p (n t)"),
             )
+
+        def multiply(first_slot, n_slots):
             acc = psum.tile([P, n_slots], F32, name="acc%d" % first_slot)
             for h in range(n_slots // C):
                 cols = slice(first_slot + h * C, first_slot + (h + 1) * C)
@@ -136,14 +139,24 @@ def tile_routed_moe_kernel(tc, xT, w, gate, offs, pos1, pos2, out):
                     start=True,
                     stop=True,
                 )
-            nc.scalar.copy(y[:, piece], acc[:])
+            return acc
 
-        tokens(0, CUT)
-        tokens(CUT, CUT)
-        tokens(2 * CUT, CUT)
-        quantize_w(wg_s[:], 3, 4)
-        tokens(3 * CUT, C)
-        tokens(3 * CUT + C, C)
+        def leave(engine_copy, acc, first_slot, n_slots):
+            engine_copy(y[:, first_slot : first_slot + n_slots], acc[:])
+
+        for first_slot in (0, CUT):
+            quantize_x(first_slot, CUT)
+            leave(nc.scalar.copy, multiply(first_slot, CUT), first_slot, CUT)
+        quantize_x(2 * CUT, CUT)
+        acc45 = multiply(2 * CUT, CUT)
+        quantize_x(7 * C, C)
+        acc7 = multiply(7 * C, C)
+        quantize_x(6 * C, C)
+        quantize_w(wg_s[:, 0:1], 6, 7)
+        acc6 = multiply(6 * C, C)
+        leave(nc.vector.tensor_copy, acc45, 2 * CUT, CUT)
+        leave(nc.vector.tensor_copy, acc7, 7 * C, C)
+        leave(nc.scalar.copy, acc6, 6 * C, C)
 
         first = keep.tile([P, T], F32, name="first")
         second = keep.tile([P, T], F32, name="second")

@@ -18,8 +18,8 @@ COPY = mybir.ActivationFunctionType.Copy
 P = 128
 PACK = 4
 SLOTS = E * C
-CUT = 256
-GATHERS = ((0, 512), (512, 1024))
+V_SLOTS = 7 * C // 2
+V_CODES = 3 * C
 HALF = T // 2
 
 
@@ -37,10 +37,9 @@ def tile_routed_moe_kernel(tc, xT, w, gate, offs, pos1, pos2, out):
         nc.sync.dma_start(offs_t[:], offs)
         planes = xT.rearrange("(p t) n -> p t n", t=PACK)
         xp = {}
-
-        def load_plane(t):
-            plane = keep.tile([P, 2 * T if t < 2 else T], F32, name="xp%d" % t)
-            nc.sync.dma_start(plane[:, 0:T], planes[:, t, :])
+        for t in range(PACK):
+            plane = keep.tile([P, T], F32, name="xp%d" % t)
+            nc.sync.dma_start(plane[:], planes[:, t, :])
             xp[t] = plane
 
         def load_w(e0, e1, name):
@@ -51,13 +50,7 @@ def tile_routed_moe_kernel(tc, xT, w, gate, offs, pos1, pos2, out):
             )
             return raw
 
-        load_plane(0)
-        load_plane(2)
-        load_plane(1)
-        load_plane(3)
-        w_raw_g = load_w(7, 8, "w_raw_g")
-        w_raw_v = load_w(0, 6, "turn_w")
-        w_raw_s = load_w(6, 7, "w_raw_s")
+        w_raw = load_w(0, E, "turn_w")
         nc.sync.dma_start(pos1_t[:], pos1)
         nc.sync.dma_start(pos2_t[:], pos2)
         gates = []
@@ -67,23 +60,24 @@ def tile_routed_moe_kernel(tc, xT, w, gate, offs, pos1, pos2, out):
             gates.append(g)
 
         y = keep.tile([P, SLOTS], F32, name="y")
-        wg_v = keep.tile([P, 6, N, PACK], BF16, name="wg_v", align_bytes=64)
-        wg_s = keep.tile([P, 2, N, PACK], BF16, name="wg_s", align_bytes=64)
+        wg = keep.tile([P, E, N, PACK], BF16, name="wg", align_bytes=64)
+        w_codes = keep.tile([P, SLOTS], U32, name="w_codes", align_bytes=64)
         w_scales = keep.tile([P, SLOTS], U8, name="w_scales", align_bytes=64)
-        xb = keep.tile([P, 2, T], BF16, name="xb", align_bytes=64)
         xg = keep.tile([P, SLOTS, PACK], BF16, name="xg", align_bytes=64)
-        g2 = keep.tile([P, 2, SLOTS], F32, name="g2")
+        g4 = keep.tile([P, PACK, V_SLOTS], F32, name="g4")
+        x_scales = keep.tile([P, SLOTS], U8, name="x_scales", align_bytes=64)
+        xc_v = keep.tile([P, V_CODES], U32, name="xc_v", align_bytes=64)
 
-        for u in range(2):
-            nc.scalar.copy(xb[:, u, :], xp[2 + u][:])
-        for t in range(2):
-            for a, b in GATHERS:
-                nc.vector.tensor_copy(g2[:, t, a:b], xp[t][:].indirect(offs_t[:, a // 16 : b // 16]))
-        for u in range(2):
-            for e in range(E):
-                nc.scalar.activation(
-                    xg[:, e * C : (e + 1) * C, 2 + u], xb[:, u, :].indirect(offs_t[:, e * (C // 16) : (e + 1) * (C // 16)]), COPY
-                )
+        xb = {}
+        for t, cast in ((0, nc.scalar.copy), (1, nc.gpsimd.tensor_copy), (2, nc.gpsimd.tensor_copy), (3, nc.scalar.copy)):
+            plane = keep.tile([P, T], BF16, name="xb%d" % t, align_bytes=64)
+            cast(plane[:], xp[t][:])
+            xb[t] = plane
+        for t in range(PACK):
+            nc.vector.tensor_copy(g4[:, t, :], xp[t][:].indirect(offs_t[:, 0 : V_SLOTS // 16]))
+        for t in (0, 3, 1, 2):
+            for a, b in [(V_SLOTS, 4 * C)] + [(e * C, (e + 1) * C) for e in range(4, E)]:
+                nc.scalar.activation(xg[:, a:b, t], xb[t][:].indirect(offs_t[:, a // 16 : b // 16]), COPY)
 
         def cast_w(engine_copy, grouped, raw):
             engine_copy(
@@ -91,72 +85,74 @@ def tile_routed_moe_kernel(tc, xT, w, gate, offs, pos1, pos2, out):
                 raw.rearrange("p e j (c i) -> p e c j i", i=4),
             )
 
-        def quantize_w(grouped, e0, e1):
+        def quantize_w(e0, e1):
             cols = slice(e0 * C, e1 * C)
             nc.vector.quantize_mx(
                 out=w_codes[:, cols].bitcast(FP8X4),
                 scales=w_scales[:, cols],
-                in_=grouped.rearrange("p e n j -> p (e n j)"),
+                in_=wg[:, e0:e1].rearrange("p e n j -> p (e n j)"),
             )
 
-        cast_w(nc.vector.tensor_copy, wg_v[:, 0:4], w_raw_v[:, 0:4])
-        cast_w(nc.vector.tensor_copy, wg_v[:, 4:6], w_raw_v[:, 4:6])
-        cast_w(nc.scalar.copy, wg_s[:, 0:1], w_raw_s[:])
-        nc.gpsimd.tensor_copy(wg_s[:, 1], w_raw_g[:, 0].rearrange("p j n -> p n j"))
-
-        for s in range(2):
-            cols = slice(s * 2 * CUT, (s + 1) * 2 * CUT)
+        def interleave(a, b):
             nc.vector.tensor_copy(
-                xg[:, cols, 0:2].rearrange("p (c i) t -> p c t i", i=4),
-                g2[:, :, cols].rearrange("p t (c i) -> p c t i", i=4),
+                xg[:, a:b].rearrange("p (c i) t -> p c t i", i=4),
+                g4[:, :, a:b].rearrange("p t (c i) -> p c t i", i=4),
             )
 
-        w_codes = keep.tile([P, SLOTS], U32, name="w_codes", align_bytes=64)
-        quantize_w(wg_v[:, 0:4], 0, 4)
-        quantize_w(wg_v[:, 4:6], 4, 6)
-        quantize_w(wg_s[:, 1:2], 7, 8)
-        x_codes = keep.tile([P, SLOTS], U32, name="x_codes", tag="turn_w", align_bytes=64)
-        x_scales = keep.tile([P, SLOTS], U8, name="x_scales", align_bytes=64)
+        def codes(e0, e1):
+            if e0 * C < V_CODES:
+                return xc_v[:, e0 * C : e1 * C].bitcast(FP8X4)
+            return xc_s[:, e0 * C - V_CODES : e1 * C - V_CODES].bitcast(FP8X4)
 
-        def quantize_x(first_slot, n_slots):
-            piece = slice(first_slot, first_slot + n_slots)
+        def quantize_x(e0, e1):
+            piece = slice(e0 * C, e1 * C)
             nc.vector.quantize_mx(
-                out=x_codes[:, piece].bitcast(FP8X4),
+                out=codes(e0, e1),
                 scales=x_scales[:, piece],
-                in_=xg[:, piece, :].rearrange("p n t -> p (n t)"),
+                in_=xg[:, piece].rearrange("p n t -> p (n t)"),
             )
 
-        def multiply(first_slot, n_slots):
-            acc = psum.tile([P, n_slots], F32, name="acc%d" % first_slot)
-            for h in range(n_slots // C):
-                cols = slice(first_slot + h * C, first_slot + (h + 1) * C)
+        def multiply(e0, e1):
+            acc = psum.tile([P, (e1 - e0) * C], F32, name="acc%d" % e0)
+            for e in range(e0, e1):
+                cols = slice(e * C, (e + 1) * C)
                 nc.tensor.matmul_mx(
-                    out=acc[:, h * C : (h + 1) * C],
+                    out=acc[:, (e - e0) * C : (e - e0 + 1) * C],
                     lhsT=w_codes[:, cols].bitcast(FP8X4),
                     lhsT_scale=w_scales[:, cols],
-                    rhs=x_codes[:, cols].bitcast(FP8X4),
+                    rhs=codes(e, e + 1),
                     rhs_scale=x_scales[:, cols],
                     start=True,
                     stop=True,
                 )
             return acc
 
-        def leave(engine_copy, acc, first_slot, n_slots):
-            engine_copy(y[:, first_slot : first_slot + n_slots], acc[:])
+        def leave(engine_copy, acc, e0, e1):
+            engine_copy(y[:, e0 * C : e1 * C], acc[:])
 
-        for first_slot in (0, CUT):
-            quantize_x(first_slot, CUT)
-            leave(nc.scalar.copy, multiply(first_slot, CUT), first_slot, CUT)
-        quantize_x(2 * CUT, CUT)
-        acc45 = multiply(2 * CUT, CUT)
-        quantize_x(7 * C, C)
-        acc7 = multiply(7 * C, C)
-        quantize_x(6 * C, C)
-        quantize_w(wg_s[:, 0:1], 6, 7)
-        acc6 = multiply(6 * C, C)
-        leave(nc.vector.tensor_copy, acc45, 2 * CUT, CUT)
-        leave(nc.vector.tensor_copy, acc7, 7 * C, C)
-        leave(nc.scalar.copy, acc6, 6 * C, C)
+        cast_w(nc.vector.tensor_copy, wg[:, 0:4], w_raw[:, 0:4])
+        cast_w(nc.vector.tensor_copy, wg[:, 4:8], w_raw[:, 4:8])
+        interleave(0, 2 * C)
+        interleave(2 * C, V_SLOTS)
+        quantize_x(0, 2)
+        quantize_x(2, 3)
+        quantize_w(0, 4)
+        quantize_w(4, 8)
+        leave(nc.scalar.copy, multiply(0, 2), 0, 2)
+        leave(nc.scalar.copy, multiply(2, 3), 2, 3)
+        xc_s = keep.tile([P, SLOTS - V_CODES], U32, name="xc_s", tag="turn_w", align_bytes=64)
+        quantize_x(3, 4)
+        acc3 = multiply(3, 4)
+        quantize_x(4, 6)
+        acc45 = multiply(4, 6)
+        quantize_x(6, 7)
+        acc6 = multiply(6, 7)
+        quantize_x(7, 8)
+        acc7 = multiply(7, 8)
+        leave(nc.vector.tensor_copy, acc3, 3, 4)
+        leave(nc.vector.tensor_copy, acc45, 4, 6)
+        leave(nc.scalar.copy, acc6, 6, 7)
+        leave(nc.scalar.copy, acc7, 7, 8)
 
         first = keep.tile([P, T], F32, name="first")
         second = keep.tile([P, T], F32, name="second")

@@ -18,8 +18,9 @@ COPY = mybir.ActivationFunctionType.Copy
 P = 128
 PACK = 4
 SLOTS = E * C
-V_SLOTS = 7 * C // 2
-V_CODES = 3 * C
+V_SLOTS = 384
+V_GATHERS = ((0, 256), (256, V_SLOTS))
+V_EXPERTS = 3
 HALF = T // 2
 
 
@@ -34,13 +35,14 @@ def tile_routed_moe_kernel(tc, xT, w, gate, offs, pos1, pos2, out):
         pos1_t = lists.tile([P, T // 16], U16, name="pos1_t")
         pos2_t = lists.tile([P, T // 16], U16, name="pos2_t")
 
-        nc.sync.dma_start(offs_t[:], offs)
         planes = xT.rearrange("(p t) n -> p t n", t=PACK)
         xp = {}
         for t in range(PACK):
             plane = keep.tile([P, T], F32, name="xp%d" % t)
             nc.sync.dma_start(plane[:], planes[:, t, :])
             xp[t] = plane
+            if t == 0:
+                nc.sync.dma_start(offs_t[:], offs)
 
         def load_w(e0, e1, name):
             raw = keep.tile([P, e1 - e0, PACK, N], F32, name=name, tag=name, align_bytes=64)
@@ -50,7 +52,8 @@ def tile_routed_moe_kernel(tc, xT, w, gate, offs, pos1, pos2, out):
             )
             return raw
 
-        w_raw = load_w(0, E, "turn_w")
+        w_lo = load_w(0, 4, "w_lo")
+        w_hi = load_w(4, 8, "turn_w")
         nc.sync.dma_start(pos1_t[:], pos1)
         nc.sync.dma_start(pos2_t[:], pos2)
         gates = []
@@ -65,23 +68,28 @@ def tile_routed_moe_kernel(tc, xT, w, gate, offs, pos1, pos2, out):
         w_scales = keep.tile([P, SLOTS], U8, name="w_scales", align_bytes=64)
         xg = keep.tile([P, SLOTS, PACK], BF16, name="xg", align_bytes=64)
         g4 = keep.tile([P, PACK, V_SLOTS], F32, name="g4")
+        x_codes_v = keep.tile([P, V_EXPERTS * C], U32, name="x_codes_v", align_bytes=64)
         x_scales = keep.tile([P, SLOTS], U8, name="x_scales", align_bytes=64)
-        xc_v = keep.tile([P, V_CODES], U32, name="xc_v", align_bytes=64)
 
-        xb = {}
-        for t, cast in ((0, nc.scalar.copy), (1, nc.gpsimd.tensor_copy), (2, nc.gpsimd.tensor_copy), (3, nc.scalar.copy)):
-            plane = keep.tile([P, T], BF16, name="xb%d" % t, align_bytes=64)
-            cast(plane[:], xp[t][:])
-            xb[t] = plane
-        for t in range(PACK):
-            nc.vector.tensor_copy(g4[:, t, :], xp[t][:].indirect(offs_t[:, 0 : V_SLOTS // 16]))
-        for t in (0, 3, 1, 2):
-            for a, b in [(V_SLOTS, 4 * C)] + [(e * C, (e + 1) * C) for e in range(4, E)]:
-                nc.scalar.activation(xg[:, a:b, t], xb[t][:].indirect(offs_t[:, a // 16 : b // 16]), COPY)
+        for a, b in V_GATHERS:
+            for t in range(PACK):
+                nc.vector.tensor_copy(g4[:, t, a:b], xp[t][:].indirect(offs_t[:, a // 16 : b // 16]))
 
-        def cast_w(engine_copy, grouped, raw):
-            engine_copy(
-                grouped.rearrange("p e (c i) j -> p e c j i", i=4),
+        for t, cast in ((0, nc.scalar.copy), (1, nc.scalar.copy), (2, nc.gpsimd.tensor_copy), (3, nc.gpsimd.tensor_copy)):
+            xb = keep.tile([P, T], BF16, name="xb%d" % t, align_bytes=64)
+            cast(xb[:], xp[t][:])
+            for a in range(V_SLOTS, SLOTS, C):
+                nc.scalar.activation(xg[:, a : a + C, t], xb[:].indirect(offs_t[:, a // 16 : (a + C) // 16]), COPY)
+
+        def interleave(a, b):
+            nc.vector.tensor_copy(
+                xg[:, a:b].rearrange("p (c i) t -> p c t i", i=4),
+                g4[:, :, a:b].rearrange("p t (c i) -> p c t i", i=4),
+            )
+
+        def cast_w(e0, e1, raw):
+            nc.vector.tensor_copy(
+                wg[:, e0:e1].rearrange("p e (c i) j -> p e c j i", i=4),
                 raw.rearrange("p e j (c i) -> p e c j i", i=4),
             )
 
@@ -93,26 +101,20 @@ def tile_routed_moe_kernel(tc, xT, w, gate, offs, pos1, pos2, out):
                 in_=wg[:, e0:e1].rearrange("p e n j -> p (e n j)"),
             )
 
-        def interleave(a, b):
-            nc.vector.tensor_copy(
-                xg[:, a:b].rearrange("p (c i) t -> p c t i", i=4),
-                g4[:, :, a:b].rearrange("p t (c i) -> p c t i", i=4),
-            )
-
-        def codes(e0, e1):
-            if e0 * C < V_CODES:
-                return xc_v[:, e0 * C : e1 * C].bitcast(FP8X4)
-            return xc_s[:, e0 * C - V_CODES : e1 * C - V_CODES].bitcast(FP8X4)
+        def x_codes(e0, e1):
+            if e0 < V_EXPERTS:
+                return x_codes_v[:, e0 * C : e1 * C].bitcast(FP8X4)
+            return x_codes_s[:, (e0 - V_EXPERTS) * C : (e1 - V_EXPERTS) * C].bitcast(FP8X4)
 
         def quantize_x(e0, e1):
             piece = slice(e0 * C, e1 * C)
             nc.vector.quantize_mx(
-                out=codes(e0, e1),
+                out=x_codes(e0, e1),
                 scales=x_scales[:, piece],
                 in_=xg[:, piece].rearrange("p n t -> p (n t)"),
             )
 
-        def multiply(e0, e1):
+        def multiply(e0, e1, engine_copy):
             acc = psum.tile([P, (e1 - e0) * C], F32, name="acc%d" % e0)
             for e in range(e0, e1):
                 cols = slice(e * C, (e + 1) * C)
@@ -120,39 +122,28 @@ def tile_routed_moe_kernel(tc, xT, w, gate, offs, pos1, pos2, out):
                     out=acc[:, (e - e0) * C : (e - e0 + 1) * C],
                     lhsT=w_codes[:, cols].bitcast(FP8X4),
                     lhsT_scale=w_scales[:, cols],
-                    rhs=codes(e, e + 1),
+                    rhs=x_codes(e, e + 1),
                     rhs_scale=x_scales[:, cols],
                     start=True,
                     stop=True,
                 )
-            return acc
-
-        def leave(engine_copy, acc, e0, e1):
             engine_copy(y[:, e0 * C : e1 * C], acc[:])
 
-        cast_w(nc.vector.tensor_copy, wg[:, 0:4], w_raw[:, 0:4])
-        cast_w(nc.vector.tensor_copy, wg[:, 4:8], w_raw[:, 4:8])
-        interleave(0, 2 * C)
-        interleave(2 * C, V_SLOTS)
+        interleave(*V_GATHERS[0])
         quantize_x(0, 2)
+        interleave(*V_GATHERS[1])
         quantize_x(2, 3)
-        quantize_w(0, 4)
-        quantize_w(4, 8)
-        leave(nc.scalar.copy, multiply(0, 2), 0, 2)
-        leave(nc.scalar.copy, multiply(2, 3), 2, 3)
-        xc_s = keep.tile([P, SLOTS - V_CODES], U32, name="xc_s", tag="turn_w", align_bytes=64)
-        quantize_x(3, 4)
-        acc3 = multiply(3, 4)
-        quantize_x(4, 6)
-        acc45 = multiply(4, 6)
-        quantize_x(6, 7)
-        acc6 = multiply(6, 7)
-        quantize_x(7, 8)
-        acc7 = multiply(7, 8)
-        leave(nc.vector.tensor_copy, acc3, 3, 4)
-        leave(nc.vector.tensor_copy, acc45, 4, 6)
-        leave(nc.scalar.copy, acc6, 6, 7)
-        leave(nc.scalar.copy, acc7, 7, 8)
+        for raw, e0 in ((w_lo, 0), (w_hi, 4)):
+            for h in (0, 2):
+                cast_w(e0 + h, e0 + h + 2, raw[:, h : h + 2])
+        for e in range(0, E, 2):
+            quantize_w(e, e + 2)
+        multiply(0, 2, nc.scalar.copy)
+        multiply(2, 3, nc.scalar.copy)
+        x_codes_s = keep.tile([P, SLOTS - V_EXPERTS * C], U32, name="x_codes_s", tag="turn_w", align_bytes=64)
+        for e0, e1, engine_copy in ((3, 4, nc.scalar.copy), (4, 6, nc.vector.tensor_copy), (6, 7, nc.scalar.copy), (7, 8, nc.scalar.copy)):
+            quantize_x(e0, e1)
+            multiply(e0, e1, engine_copy)
 
         first = keep.tile([P, T], F32, name="first")
         second = keep.tile([P, T], F32, name="second")

@@ -18,7 +18,7 @@ COPY = mybir.ActivationFunctionType.Copy
 P = 128
 PACK = 4
 SLOTS = E * C
-V_SLOTS = 384
+V_SLOTS = 416
 V_GATHERS = ((0, 256), (256, V_SLOTS))
 V_EXPERTS = 3
 HALF = T // 2
@@ -78,8 +78,8 @@ def tile_routed_moe_kernel(tc, xT, w, gate, offs, pos1, pos2, out):
         for t, cast in ((0, nc.scalar.copy), (1, nc.scalar.copy), (2, nc.gpsimd.tensor_copy), (3, nc.gpsimd.tensor_copy)):
             xb = keep.tile([P, T], BF16, name="xb%d" % t, align_bytes=64)
             cast(xb[:], xp[t][:])
-            for a in range(V_SLOTS, SLOTS, C):
-                nc.scalar.activation(xg[:, a : a + C, t], xb[:].indirect(offs_t[:, a // 16 : (a + C) // 16]), COPY)
+            for a, b in [(V_SLOTS, 4 * C)] + [(e * C, (e + 1) * C) for e in range(4, E)]:
+                nc.scalar.activation(xg[:, a:b, t], xb[:].indirect(offs_t[:, a // 16 : b // 16]), COPY)
 
         def interleave(a, b):
             nc.vector.tensor_copy(

@@ -19,7 +19,7 @@ P = 128
 PACK = 4
 SLOTS = E * C
 V_SLOTS = 416
-V_GATHERS = ((0, 256), (256, V_SLOTS))
+V_PIECES = ((0, 256), (256, V_SLOTS))
 V_EXPERTS = 3
 HALF = T // 2
 
@@ -71,8 +71,8 @@ def tile_routed_moe_kernel(tc, xT, w, gate, offs, pos1, pos2, out):
         x_codes_v = keep.tile([P, V_EXPERTS * C], U32, name="x_codes_v", align_bytes=64)
         x_scales = keep.tile([P, SLOTS], U8, name="x_scales", align_bytes=64)
 
-        for a, b in V_GATHERS:
-            for t in range(PACK):
+        for t in range(PACK):
+            for a, b in ((0, V_SLOTS),) if t < PACK - 1 else V_PIECES:
                 nc.vector.tensor_copy(g4[:, t, a:b], xp[t][:].indirect(offs_t[:, a // 16 : b // 16]))
 
         for t, cast in ((0, nc.scalar.copy), (1, nc.scalar.copy), (2, nc.gpsimd.tensor_copy), (3, nc.gpsimd.tensor_copy)):
@@ -129,9 +129,9 @@ def tile_routed_moe_kernel(tc, xT, w, gate, offs, pos1, pos2, out):
                 )
             engine_copy(y[:, e0 * C : e1 * C], acc[:])
 
-        interleave(*V_GATHERS[0])
+        interleave(*V_PIECES[0])
+        interleave(*V_PIECES[1])
         quantize_x(0, 2)
-        interleave(*V_GATHERS[1])
         quantize_x(2, 3)
         for raw, e0 in ((w_lo, 0), (w_hi, 4)):
             for h in (0, 2):
@@ -141,7 +141,7 @@ def tile_routed_moe_kernel(tc, xT, w, gate, offs, pos1, pos2, out):
         multiply(0, 2, nc.scalar.copy)
         multiply(2, 3, nc.scalar.copy)
         x_codes_s = keep.tile([P, SLOTS - V_EXPERTS * C], U32, name="x_codes_s", tag="turn_w", align_bytes=64)
-        for e0, e1, engine_copy in ((3, 4, nc.scalar.copy), (4, 6, nc.vector.tensor_copy), (6, 7, nc.scalar.copy), (7, 8, nc.scalar.copy)):
+        for e0, e1, engine_copy in ((4, 6, nc.vector.tensor_copy), (3, 4, nc.scalar.copy), (6, 7, nc.scalar.copy), (7, 8, nc.scalar.copy)):
             quantize_x(e0, e1)
             multiply(e0, e1, engine_copy)
 

from contextlib import ExitStack

import concourse.mybir as mybir

K, T, E, C, N = 512, 512, 8, 128, 128
FLOPS = 2 * K * N * E * C

F32 = mybir.dt.float32
BF16 = mybir.dt.bfloat16
U32 = mybir.dt.uint32
U16 = mybir.dt.uint16
U8 = mybir.dt.uint8
FP8X4 = mybir.dt.float8_e4m3fn_x4
MULT = mybir.AluOpType.mult
ADD = mybir.AluOpType.add
COPY = mybir.ActivationFunctionType.Copy

P = 128
PACK = 4
SLOTS = E * C
V_SLOTS = 416
V_PIECES = ((0, 256), (256, V_SLOTS))
V_EXPERTS = 3
HALF = T // 2


def tile_routed_moe_kernel(tc, xT, w, gate, offs, pos1, pos2, out):
    nc = tc.nc
    with ExitStack() as ctx:
        lists = ctx.enter_context(tc.tile_pool(name="lists", bufs=1))
        keep = ctx.enter_context(tc.tile_pool(name="keep", bufs=1))
        psum = ctx.enter_context(tc.psum_pool(name="psum", bufs=1))

        offs_t = lists.tile([P, SLOTS // 16], U16, name="offs_t")
        pos1_t = lists.tile([P, T // 16], U16, name="pos1_t")
        pos2_t = lists.tile([P, T // 16], U16, name="pos2_t")

        planes = xT.rearrange("(p t) n -> p t n", t=PACK)
        xp = {}
        for t in range(PACK):
            plane = keep.tile([P, T], F32, name="xp%d" % t)
            nc.sync.dma_start(plane[:], planes[:, t, :])
            xp[t] = plane
            if t == 0:
                nc.sync.dma_start(offs_t[:], offs)

        def load_w(e0, e1, name):
            raw = keep.tile([P, e1 - e0, PACK, N], F32, name=name, tag=name, align_bytes=64)
            nc.sync.dma_start(
                raw[:].rearrange("p e j n -> p e (j n)"),
                w[e0:e1].rearrange("e (p j) n -> p e (j n)", j=PACK),
            )
            return raw

        w_lo = load_w(0, 4, "w_lo")
        w_hi = load_w(4, 8, "turn_w")
        nc.sync.dma_start(pos1_t[:], pos1)
        nc.sync.dma_start(pos2_t[:], pos2)
        gates = []
        for r in range(2):
            g = keep.tile([P, T], F32, name="gate%d" % r)
            nc.sync.dma_start(g[:], gate[r])
            gates.append(g)

        y = keep.tile([P, SLOTS], F32, name="y")
        wg = keep.tile([P, E, N, PACK], BF16, name="wg", align_bytes=64)
        w_codes = keep.tile([P, SLOTS], U32, name="w_codes", align_bytes=64)
        w_scales = keep.tile([P, SLOTS], U8, name="w_scales", align_bytes=64)
        xg = keep.tile([P, SLOTS, PACK], BF16, name="xg", align_bytes=64)
        g4 = keep.tile([P, PACK, V_SLOTS], F32, name="g4")
        x_codes_v = keep.tile([P, V_EXPERTS * C], U32, name="x_codes_v", align_bytes=64)
        x_scales = keep.tile([P, SLOTS], U8, name="x_scales", align_bytes=64)

        for t in range(PACK):
            for a, b in ((0, V_SLOTS),) if t < PACK - 1 else V_PIECES:
                nc.vector.tensor_copy(g4[:, t, a:b], xp[t][:].indirect(offs_t[:, a // 16 : b // 16]))

        for t, cast in ((0, nc.scalar.copy), (1, nc.scalar.copy), (2, nc.gpsimd.tensor_copy), (3, nc.gpsimd.tensor_copy)):
            xb = keep.tile([P, T], BF16, name="xb%d" % t, align_bytes=64)
            cast(xb[:], xp[t][:])
            for a, b in [(V_SLOTS, 4 * C)] + [(e * C, (e + 1) * C) for e in range(4, E)]:
                nc.scalar.activation(xg[:, a:b, t], xb[:].indirect(offs_t[:, a // 16 : b // 16]), COPY)

        def interleave(a, b):
            nc.vector.tensor_copy(
                xg[:, a:b].rearrange("p (c i) t -> p c t i", i=4),
                g4[:, :, a:b].rearrange("p t (c i) -> p c t i", i=4),
            )

        def cast_w(e0, e1, raw):
            nc.vector.tensor_copy(
                wg[:, e0:e1].rearrange("p e (c i) j -> p e c j i", i=4),
                raw.rearrange("p e j (c i) -> p e c j i", i=4),
            )

        def quantize_w(e0, e1):
            cols = slice(e0 * C, e1 * C)
            nc.vector.quantize_mx(
                out=w_codes[:, cols].bitcast(FP8X4),
                scales=w_scales[:, cols],
                in_=wg[:, e0:e1].rearrange("p e n j -> p (e n j)"),
            )

        def x_codes(e0, e1):
            if e0 < V_EXPERTS:
                return x_codes_v[:, e0 * C : e1 * C].bitcast(FP8X4)
            return x_codes_s[:, (e0 - V_EXPERTS) * C : (e1 - V_EXPERTS) * C].bitcast(FP8X4)

        def quantize_x(e0, e1):
            piece = slice(e0 * C, e1 * C)
            nc.vector.quantize_mx(
                out=x_codes(e0, e1),
                scales=x_scales[:, piece],
                in_=xg[:, piece].rearrange("p n t -> p (n t)"),
            )

        def multiply(e0, e1, engine_copy):
            acc = psum.tile([P, (e1 - e0) * C], F32, name="acc%d" % e0)
            for e in range(e0, e1):
                cols = slice(e * C, (e + 1) * C)
                nc.tensor.matmul_mx(
                    out=acc[:, (e - e0) * C : (e - e0 + 1) * C],
                    lhsT=w_codes[:, cols].bitcast(FP8X4),
                    lhsT_scale=w_scales[:, cols],
                    rhs=x_codes(e, e + 1),
                    rhs_scale=x_scales[:, cols],
                    start=True,
                    stop=True,
                )
            engine_copy(y[:, e0 * C : e1 * C], acc[:])

        interleave(*V_PIECES[0])
        interleave(*V_PIECES[1])
        quantize_x(0, 2)
        quantize_x(2, 3)
        for raw, e0 in ((w_lo, 0), (w_hi, 4)):
            for h in (0, 2):
                cast_w(e0 + h, e0 + h + 2, raw[:, h : h + 2])
        for e in range(0, E, 2):
            quantize_w(e, e + 2)
        multiply(0, 2, nc.scalar.copy)
        multiply(2, 3, nc.scalar.copy)
        x_codes_s = keep.tile([P, SLOTS - V_EXPERTS * C], U32, name="x_codes_s", tag="turn_w", align_bytes=64)
        for e0, e1, engine_copy in ((4, 6, nc.vector.tensor_copy), (3, 4, nc.scalar.copy), (6, 7, nc.scalar.copy), (7, 8, nc.scalar.copy)):
            quantize_x(e0, e1)
            multiply(e0, e1, engine_copy)

        first = keep.tile([P, T], F32, name="first")
        second = keep.tile([P, T], F32, name="second")
        total = keep.tile([P, T], F32, name="total")
        nc.vector.tensor_tensor(first[:], y[:].indirect(pos1_t[:]), gates[0][:], MULT)
        for h in range(2):
            tok = slice(h * HALF, (h + 1) * HALF)
            lst = slice(h * (HALF // 16), (h + 1) * (HALF // 16))
            nc.vector.tensor_tensor(second[:, tok], y[:].indirect(pos2_t[:, lst]), gates[1][:, tok], MULT)
        for h in range(2):
            tok = slice(h * HALF, (h + 1) * HALF)
            nc.vector.tensor_tensor(total[:, tok], first[:, tok], second[:, tok], ADD)
            nc.sync.dma_start(out[:, tok], total[:, tok])
